import numpy as np, ml_dtypes
CORES = [35,38,43,46]
N = 4
import mx_ref
BF = ml_dtypes.bfloat16
def gentries(a):
    return np.ascontiguousarray(a.reshape(8, 16, -1).transpose(0, 2, 1)).reshape(8, -1)
def gtable(e):
    e = np.asarray(e); return np.ascontiguousarray(e.reshape(8, -1, 16).transpose(0, 2, 1)).reshape(128, -1).astype(np.int32)
def gcols(t, e):
    v = np.concatenate([t.reshape(8, 16, -1, 4), np.zeros((8, 16, 1, 4), BF)], axis=2)
    return np.ascontiguousarray(np.stack([v[g][:, e[g]] for g in range(8)])).reshape(128, -1)
def tile(rs):
    return np.stack(rs, axis=2).reshape(128, -1).astype(BF)
def pick(q, e):
    c = np.concatenate([q[0].reshape(128, -1, 4), np.zeros((128, 1, 4), np.uint8)], axis=1); s = np.concatenate([q[1], np.ones((16, 1), np.uint8)], axis=1)
    return (np.ascontiguousarray(c[:, e].reshape(128, -1)), np.ascontiguousarray(s[:, e]))
def join(*qs):
    return (np.concatenate([q[0] for q in qs], axis=1), np.concatenate([q[1] for q in qs], axis=1))
def put(q, e, v):
    c, s = q[0].reshape(128, -1, 4).copy(), q[1].copy(); c[:, e] = v[0].reshape(128, -1, 4); s[:, e] = v[1]
    return (c.reshape(128, -1), s)
def pk(c, s):
    return (np.ascontiguousarray(c), mx_ref.live(s))
def emit(q):
    return q[0], q[1]
def packed(v, rng):
    q = [mx_ref.quantize(np.ascontiguousarray(v[r])) for r in range(N)]
    return np.stack([a for a, b in q]), np.stack([mx_ref.plane(b, rng) for a, b in q])
def values_of_codes():
    e, c = np.zeros((128, 128, 4), np.float32), np.zeros((128, 2, 4), np.uint8)
    e[np.arange(128), np.arange(128), 0] = 1
    c[:127, :, 0] = np.arange(256).reshape(2, 128).T[:127]
    return mx_ref.matmul(mx_ref.quantize(e.reshape(128, 512).astype(BF)), (c.reshape(128, 8), np.full((16, 2), 127, np.uint8))).T.reshape(-1).astype(np.float64)
CODE_VALUE, SCALE_VALUE = values_of_codes(), 2.0 ** (np.arange(256) - 127.0)
def decode(q):
    return (CODE_VALUE[q[0]].reshape(16, 8, -1, 4) * SCALE_VALUE[q[1]][:, None, :, None] + 0.0).reshape(128, -1).astype(np.float32)
def f(rng, *shape):
    return mx_ref.flush((rng.standard_normal(shape, dtype=np.float32) * np.exp2(rng.integers(-2, 3, shape[:-1] + (1,)))).astype(BF))
def wide(rng, *shape, cols=0):
    v = rng.standard_normal(shape, dtype=np.float32) * np.exp2(rng.integers(-12, 13, shape)).astype(np.float32)
    if cols: v *= np.repeat(np.exp2(rng.integers(-cols, cols + 1, shape[:-2] + (1, shape[-1] // 4))) * (rng.random(shape[:-2] + (1, shape[-1] // 4)) > 0.0625), 4, axis=-1).astype(np.float32)
    return mx_ref.flush(v.astype(BF))
C, M, R = 384, 160, 3
SH = (N, 8, 2, C, 4)
def numbers_of(rng):
    return {"x": np.array(f(rng, N, 128, 4 * C)), "u": np.array(f(rng, N, 128, 512)), "v": np.array(f(rng, N, 128, 512))}
def lists_of(e, c, a):
    return {"al": np.stack([gtable(e[r]) for r in range(N)]), "nx": np.stack([gtable((512 * c + a)[r].reshape(8, 8 * C)) for r in range(N)])}
def lists(rng):
    return lists_of(rng.integers(0, C, (N, 8, C)), rng.integers(0, 5, SH), rng.integers(0, C, SH))
def layers(rng, still=0):
    w = np.array(f(rng, N, 128, 2048)).reshape(N, 8, 16, 4, 8, 16, 4)
    w[:, :, :still] = 0
    w[:, :, :, :, :, :still] = 0
    return w
def weights(rng, w):
    c, s = packed(np.ascontiguousarray(w).reshape(N, 128, 2048), rng)
    return {"wc": c, "ws": s}
def setup_inputs(rng):
    return {**numbers_of(rng), **lists(rng), **weights(rng, layers(rng))}
def setup_inputs_near(rng):
    d = numbers_of(rng)
    x = d["x"].reshape(N, 8, 16, C, 4)
    u = d["u"].reshape(N, 128, 128, 4)
    o = rng.permutation(N) % 2
    x[:, :, :8] = 0
    u[:, :, ::16] = 0
    u[:, :, 1::16] = 0
    for r in range(N):
        k = 2.0 ** -30 if o[r] == 0 else 1.0
        s = rng.integers(-1, 2, (8, 2, C)) * k
        for g in rng.permutation(8)[:4]: s[g, :, rng.integers(C)] = 2.0 ** 14 * rng.choice([-1.0, 1.0], 2)
        x[r, :, :2, :, 0] = s.astype(np.float32).astype(BF)
        t = np.where(s[:, 0] == 0, rng.integers(-1, 2, (8, C)), 0) * k
        x[r, :, 2, :, 0] = (1.125 * t).astype(np.float32).astype(BF)
        x[r, :, 3, :, 0] = (-t).astype(np.float32).astype(BF)
        for h in [0, 16, 32, 48, 64, 80, 96, 112, 1, 17]:
            u[r, h, h, 0] = k
            u[r, h - h % 16 + 2, h, 0] = 1.125 * k
            u[r, h - h % 16 + 3, h, 0] = 1.25 * k
    return {"x": x.reshape(N, 128, 4 * C), "u": u.reshape(N, 128, 512), "v": d["v"], **lists(rng), **weights(rng, layers(rng, 8))}
def setup_inputs_chain(rng):
    d = numbers_of(rng)
    e = rng.permutation(N)
    c = rng.integers(0, 5, SH)
    i = np.arange(4)
    c[e[0]] = rng.integers(1, 5, SH[1:])
    c[e[1]] = 0
    c[e[2]] = np.where(np.arange(8)[:, None] <= 2 * i, i + 1, 0)[:, None, None, :]
    c[e[3]][:, 0] = 0
    c[e[3]][:, 1] = rng.integers(1, 5, (8, C, 4))
    return {**d, **lists_of(rng.integers(0, C, (N, 8, C)), c, rng.integers(0, C, SH)), **weights(rng, layers(rng))}
def setup_inputs_twice(rng):
    d = numbers_of(rng)
    s = 2.0 ** -rng.integers(8, 15, (N, 16, C, 32)) * (1.125 + 0.25 * rng.integers(0, 4, (N, 16, C, 32)))
    s[:, :, :, 4] = 2.0 ** -rng.integers(8, 12, (N, 16, C)) * (1.125 + 0.25 * rng.integers(0, 4, (N, 16, C)))
    np.put_along_axis(s, rng.integers(8, 32, (N, 16, C, 1)), 1.96875, axis=3)
    s = s * rng.choice([-1.0, 1.0], s.shape)
    s[:, :, :, 0] = 0.125 * s[:, :, :, 4]
    s = s * np.exp2(rng.integers(10, 13, (N, 16, C, 1)))
    x = np.ascontiguousarray(s.reshape(N, 16, C, 8, 4).transpose(0, 1, 3, 2, 4)).reshape(N, 128, 4 * C)
    u = d["u"].reshape(N, 128, 128, 4)
    u[:, :, ::16] = 0
    for h in range(0, 128, 16):
        u[:, h, h, 0] = 1.0
        u[:, h + 1, h, 0] = -0.125
    w = np.array(mx_ref.flush((layers(rng).astype(np.float32) * np.float32(2.0 ** -12)).astype(BF))).reshape(N, 128, 4, 128, 4)
    i = np.arange(128)
    for b in range(4): w[:, i, b, i, b] = -1.0
    return {"x": x.astype(np.float32).astype(BF), "u": u.reshape(N, 128, 512), "v": d["v"], **lists(rng), **weights(rng, w)}
def setup_inputs_ends(rng):
    d = numbers_of(rng)
    e = rng.permutation(N)
    x = d["x"].reshape(N, 8, 16, C, 4)
    u = d["u"].reshape(N, 128, 128, 4)
    v = d["v"].reshape(N, 128, 128, 4)
    t = np.clip(rng.integers(-C, 2 * C, (N, 8, C)), 0, C - 1)
    c = 4 * rng.integers(0, 2, SH)
    a = np.clip(rng.integers(-C, 2 * C, SH), 0, C - 1)
    t[e[0]], c[e[0]], a[e[0]] = C - 1, 4, C - 1
    t[e[1]], c[e[1]], a[e[1]] = 0, 0, 0
    u[:, :, ::16] = 0
    u[:, :, 1::16] = 0
    for i in range(N):
        r = e[i]
        s = rng.integers(-1, 2, (8, C)) * 1.0
        s[rng.permutation(8)[:2]] = rng.choice([-1.0, 1.0], (2, 1))
        s = s * (2.0 ** -30 if i % 2 else 2.0 ** 14)
        x[r, :, :8] = s[:, None, :, None].astype(np.float32).astype(BF)
        for h in [0, 16, 32, 48, 64, 80, 96, 112, 1, 17]: u[r, h - h % 16:h - h % 16 + 8, h] = 2.0 ** -30 if i % 2 else 2.0 ** 30
    x[e[0]] = (2.0 ** 14 * rng.choice([-1.0, 1.0], (C, 1))).astype(np.float32).astype(BF)
    u[e[0]] = (2.0 ** 30 * rng.choice([-1.0, 1.0], (128, 1))).astype(np.float32).astype(BF)
    v[e[0]] = (2.0 ** 30 * rng.choice([-1.0, 1.0], (128, 1))).astype(np.float32).astype(BF)
    w = layers(rng, 8)
    w[e[0]][:, 8:, :, :, 8:] = 8
    w[e[1]] = 0
    v = (np.where(v < 0, -1.0, 1.0) * np.where(rng.permutation(N) % 2, 2.0 ** -30, 2.0 ** 30)[:, None, None, None]).astype(np.float32).astype(BF)
    return {"x": x.reshape(N, 128, 4 * C), "u": u.reshape(N, 128, 512), "v": v.reshape(N, 128, 512), **lists_of(t, c, a), **weights(rng, w)}
def setup_inputs_spread(rng):
    d = setup_inputs(rng)
    d["x"] = mx_ref.flush((wide(rng, N, 128, 4 * C, cols=6).astype(np.float32) * np.float32(2.0 ** -7)).astype(BF))
    return d
def check_inputs(d):
    b = []
    for k, most in (("x", 2.0 ** 14), ("u", 2.0 ** 30), ("v", 2.0 ** 30)):
        a = np.abs(d[k].astype(np.float32))
        if not (np.isfinite(a).all() and ((a == 0) | (a >= 2.0 ** -30) & (a <= most)).all()): b.append("a value of " + k)
    if not ((d["al"] >= 0) & (d["al"] < C)).all(): b.append("an entry of al")
    if not ((d["nx"] >= 0) & (d["nx"] < 2560) & (d["nx"] % 512 < C)).all(): b.append("an entry of nx")
    none, least, most = [emit(mx_ref.quantize(np.full((128, 16), k, np.float32).astype(BF)))[1][0, 0] for k in (0.0, 2.0 ** -30, 2.0 ** 30)]
    for r in range(N):
        if ((d["wc"][r] == 0x7F) | (d["wc"][r] == 0xFF)).any(): b.append("wc: a code that is no number")
        s = mx_ref.live(d["ws"][r])
        if ((s != none) & ((s < least) | (s > most))).any(): b.append("ws: a scale out of range")
        w = np.abs(decode(pk(d["wc"][r], d["ws"][r])).astype(np.float64)).reshape(128, 512, 4)
        if not (np.sum(w, axis=(0, 2)) <= 2048).all(): b.append("a column of W adds up to more than 2048")
    return b
def reference(x, u, v, al, nx, wc, ws):
    qu = [mx_ref.quantize(u[r]) for r in range(N)]
    lay = [pk(wc[r], ws[r]) for r in range(N)]
    now = [x[r] for r in range(N)]
    ad = np.stack([gentries(al[r]) for r in range(N)])
    follow = [gentries(nx[r]) for r in range(N)]
    for t in range(R):
        made = []
        for r in range(N):
            q = mx_ref.quantize(now[r])
            s = mx_ref.matmul(qu[r], q)
            edge = 2 * (s[1] > 0) + (s[17] > 0)
            on = np.ones(C, bool)
            for g in range(8):
                bit = s[16 * g][ad[r, g]] > 0
                n = follow[r][g][4 * C * bit + 4 * ad[r, g] + edge]
                ad[r, g] = np.where(on, n % 512, ad[r, g])
                on = on & (n >= 512)
                edge = np.where(on, n // 512 - 1, 0)
            made.append(mx_ref.quantize(gcols(decode(q).astype(BF), ad[r])))
        ad[:, :, C - M:] = np.roll(ad[:, :, C - M:], 1, axis=0)
        for r in range(N):
            q = join(pick(made[r], np.arange(C - M)), pick(made[r - 1], np.arange(C - M, C)))
            own = decode(q)
            now[r] = tile([mx_ref.matmul(pick(lay[r], np.arange(128 * b, 128 * b + 128)), q) * np.float32(0.015625) + own[:, b::4] for b in range(4)])
    y, oa = np.zeros((N, 128, C), np.float32), np.zeros((N, 8, C), np.float32)
    oc, osc = np.zeros((N, 128, 4 * C), np.uint8), np.zeros((N, 16, C), np.uint8)
    for r in range(N):
        q = mx_ref.quantize(now[r])
        y[r] = mx_ref.matmul(mx_ref.quantize(v[r]), q)
        oa[r] = ad[r]
        oc[r], osc[r] = emit(q)
    return {"y": y, "oa": oa, "oc": oc, "osc": osc}

@@ -1,0 +1,467 @@
+from concourse.mybir import dt, AluOpType, ActivationFunctionType
+
+CODES = "float8_e4m3fn_x4"
+C, NO, NR, ROUNDS = 384, 224, 160, 3
+PARTS = ((0, NO), (NO, C))
+Q2 = (0, 4, 8, 13)
+EVEN0, ODD0 = 13, 4
+NCH = 28
+EDGE_ROWS = (4, 6)
+
+_F = "float32"
+SCRATCH = {
+    "NX": ("sbuf", [128, 192], "int32"), "CI": ("sbuf", [128, 192], "int32"), "NI": ("sbuf", [128, 192], "int32"),
+    "NT": ("sbuf", [128, 192], "int32"), "ND": ("sbuf", [128, 192], _F), "AT": ("sbuf", [128, 48], _F), "NF": ("sbuf", [128, 192], _F),
+    "U4": ("sbuf", [128, 192], _F), "UU": ("sbuf", [128, 192], _F), "UT": ("sbuf", [128, 192], _F), "V2": ("sbuf", [128, 192], _F),
+    "V4": ("sbuf", [128, 192], _F), "V3": ("sbuf", [128, 192], _F), "VV": ("sbuf", [128, 192], _F),
+    "PE0": ("sbuf", [128, 192], _F), "PO0": ("sbuf", [128, 192], _F), "PE1": ("sbuf", [128, 96], _F), "PO1": ("sbuf", [128, 96], _F),
+    "YE": ("sbuf", [128, 192], _F), "YO": ("sbuf", [128, 192], _F), "FE": ("sbuf", [128, 192], _F), "FD": ("sbuf", [128, 192], _F),
+    "WE": ("sbuf", [128, 192], _F), "WO": ("sbuf", [128, 192], _F),
+    "TAB": ("sbuf", [128, 768], _F), "D0": ("sbuf", [128, 768], _F), "D1": ("sbuf", [128, 768], _F),
+    "TW": ("sbuf", [128, 776], _F), "RO": ("sbuf", [128, 256], _F), "RR": ("sbuf", [128, 192], _F),
+    "EO": ("sbuf", [128, 256], "bfloat16"), "ER": ("sbuf", [128, 192], "bfloat16"),
+    "CH": ("sbuf", [128, 32 * NCH], _F), "CE": ("sbuf", [128, 32 * NCH], "bfloat16"),
+    "MA": ("sbuf", [128, NCH], _F), "MB": ("sbuf", [128, NCH], _F),
+    "MM": ("sbuf", [128, 2 * NCH], "int32"), "YY": ("sbuf", [128, NCH], "int32"),
+    "GG": ("sbuf", [128, 16 * NCH], _F), "XS": ("sbuf", [128, 16 * NCH], _F), "SUM": ("sbuf", [128, NCH], _F),
+    "PI": ("sbuf", [128, 1], "int32"), "P15": ("sbuf", [128, 1], "int32"), "PU": ("sbuf", [128, 1], "int32"),
+    "P31": ("sbuf", [128, 1], "int32"), "PUF": ("sbuf", [128, 1], _F), "PLF": ("sbuf", [128, 1], _F), "PHF": ("sbuf", [128, 1], _F),
+    "E3": ("sbuf", [128, 1], "int32"), "E4": ("sbuf", [128, 1], "int32"), "KC": ("sbuf", [128, 4], _F),
+    "LP": ("sbuf", [128, 8], "int32"), "LPU": ("sbuf", [128, 8], "uint16"),
+    "ALI": ("sbuf", [128, 24], "int32"), "OAF": ("sbuf", [128, 32], _F), "OAT": ("sbuf", [128, 32], _F),
+    "L2O": ("sbuf", [128, 16], "uint16"), "L2R": ("sbuf", [128, 16], "uint16"),
+    "CT": ("sbuf", [128, 2048], "bfloat16"), "CTc": ("sbuf", [128, 512], CODES), "CTs": ("sbuf", [128, 512], "uint8"),
+    "UB": ("sbuf", [128, 512], "bfloat16"), "Uc": ("sbuf", [128, 128], CODES), "Us": ("sbuf", [128, 128], "uint8"),
+    "Pc": ("sbuf", [128, 128], CODES), "Ps": ("sbuf", [128, 128], "uint8"),
+    "VB": ("sbuf", [128, 512], "bfloat16"), "Vc": ("sbuf", [128, 128], CODES), "Vs": ("sbuf", [128, 128], "uint8"),
+    "Wc": ("sbuf", [128, 512], CODES), "Ws": ("sbuf", [128, 512], "uint8"),
+    "X": ("sbuf", [128, 4 * C], "bfloat16"), "FO": ("sbuf", [128, 4 * C], "bfloat16"), "FP": ("sbuf", [128, 4 * C], "bfloat16"),
+    "ZO": ("sbuf", [128, 4 * NO], "bfloat16"), "ZR": ("sbuf", [128, 4 * NR], "bfloat16"),
+    "ZOc": ("sbuf", [128, NO], CODES), "ZOs": ("sbuf", [128, NO], "uint8"),
+    "ZRc": ("sbuf", [128, NR], CODES), "ZRs": ("sbuf", [128, NR], "uint8"),
+    "Y": ("sbuf", [128, C], _F),
+}
+for _t in range(ROUNDS + 1):
+    SCRATCH["Qc%d" % _t] = ("sbuf", [128, C], CODES)
+    SCRATCH["Qs%d" % _t] = ("sbuf", [128, C], "uint8")
+    SCRATCH["AL%d" % _t] = ("sbuf", [128, NCH], _F)
+for _t in range(ROUNDS):
+    SCRATCH["Ac%d" % _t] = ("sbuf", [128, C], CODES)
+    SCRATCH["As%d" % _t] = ("sbuf", [128, C], "uint8")
+    SCRATCH["LO%d" % _t] = ("sbuf", [128, 16], "uint16")
+    SCRATCH["LS%d" % _t] = ("sbuf", [128, 12], "uint16")
+    SCRATCH["LR%d" % _t] = ("sbuf", [128, 12], "uint16")
+for _t in range(8):
+    SCRATCH["pb%d" % _t] = ("psum", [128, 512], _F)
+SEMAPHORES = ["cv", "cs", "ct", "cg", "sent"] + ["d%d" % i for i in range(48)] + ["q%d%d" % (t, h) for t in range(ROUNDS) for h in range(2)] + ["l%d" % t for t in range(ROUNDS)]
+
+
+def rank_program(g, core, T, topo):
+    rank = T.rank_of(core)
+    if rank is None:
+        return
+    n = len(T.cores)
+    nxt, prv = T.cores[(rank + 1) % n], T.cores[(rank - 1) % n]
+    n_in = len(topo.engines(prv, core))
+    rid, pid = topo.addr(nxt)[0], topo.addr(nxt)[1]
+    A = AluOpType
+    ACT = ActivationFunctionType
+    queue = {"v": g.vector, "s": g.scalar, "t": g.tensor, "g": g, "y": g.sync}
+    count, seen, hist, need_end = {}, {}, {}, {}
+
+    def view(name, c0, c1, step=1, p0=0, p1=128):
+        buf = T[name]
+        if step != 1:
+            ap = buf[p0:p1, c0:c1:step]
+        elif (p0, p1) == (0, 128):
+            ap = buf[:, c0:c1]
+        else:
+            ap = buf[p0:p1, c0:c1]
+        return (ap, (name, p0, p1, c0, c1, step))
+
+    def w(name, a=0, b=None, step=1):
+        return view(name, a, T[name].shape[1] if b is None else b, step)
+
+    def meet(a, b):
+        if a[1] >= b[2] or b[1] >= a[2] or a[3] >= b[4] or b[3] >= a[4]:
+            return False
+        return not (a[5] == b[5] and a[5] > 1 and (a[3] - b[3]) % a[5])
+
+    def waits(q, reads, writes):
+        need = {}
+        for kind, rects in (("r", reads), ("w", writes)):
+            for r in rects:
+                bank = r[0].startswith("pb")
+                for hk, hq, hsem, hval, hr in hist.get(r[0], []):
+                    if kind == "r" and hk == "r" and not (bank and hq != q):
+                        continue
+                    if kind == "w" and hq == q and q in "vstg" and not hsem.startswith("d") and (hk == "r" or q == "t"):
+                        continue
+                    if bank or meet(r, hr):
+                        need[hsem] = max(need.get(hsem, 0), hval)
+        for s in sorted(need):
+            if seen.get((q, s), 0) < need[s]:
+                queue[q].wait_ge(T.sem[s], need[s])
+                seen[(q, s)] = need[s]
+                need_end[s] = max(need_end.get(s, 0), need[s])
+
+    def note(q, sem, val, reads, writes):
+        for kind, rects in (("r", reads), ("w", writes)):
+            for r in rects:
+                lst = hist.setdefault(r[0], [])
+                if kind == "w" and r[5] == 1:
+                    lst[:] = [h for h in lst if not (h[4][1] >= r[1] and h[4][2] <= r[2] and h[4][3] >= r[3] and h[4][4] <= r[4] and h[1] == q)]
+                lst.append((kind, q, sem, val, r))
+
+    def op(q, call, reads, writes):
+        reads = [a[1] for a in reads]
+        writes = [a[1] for a in writes]
+        waits(q, reads, writes)
+        sem = "c" + q
+        count[sem] = count.get(sem, 0) + 1
+        call(queue[q]).then_inc(T.sem[sem], 1)
+        note(q, sem, count[sem], reads, writes)
+
+    n_dma = [0]
+
+    def dma(q, out, in_, reads=(), writes=()):
+        reads, writes = list(reads), list(writes)
+        waits(q, reads, writes)
+        sem = "d%d" % n_dma[0]
+        n_dma[0] += 1
+        count[sem] = 16
+        queue[q].dma_start(out, in_).then_inc(T.sem[sem], 16)
+        note(q, sem, 16, reads, writes)
+
+    def load(q, name, src, c0=0, c1=None):
+        v = w(name, c0, c1)
+        dma(q, v[0].bitcast(dt.uint8) if name == "Wc" else v[0], src, (), [v[1]])
+
+    def lands(name, c0, c1, sem, val):
+        hist.setdefault(name, []).append(("w", "far", sem, val, (name, 0, 128, c0, c1, 1)))
+        count[sem] = max(count.get(sem, 0), val)
+
+    def send(out, in_, rect, sem):
+        waits("g", [rect], [])
+        count["sent"] = count.get("sent", 0) + len(topo.engines(core, nxt))
+        g.remote_dma(out, in_, T.sem[sem], T.sem.sent, pid, rid, topo.mask(core, nxt))
+
+    def fill(ap, val):
+        op("v", lambda e: e.memset(ap[0], val), [], [ap])
+
+    def act(out, in_, func=ACT.Copy, scale=1.0, bias=0.0):
+        op("s", lambda e: e.activation(out[0], in_[0], func, bias=bias, scale=scale), [in_], [out])
+
+    def copy(q, out, in_, scale=None):
+        if q == "s":
+            act(out, in_, ACT.Copy, 1.0 if scale is None else scale)
+        elif scale is None:
+            op(q, lambda e: e.tensor_copy(out[0], in_[0]), [in_], [out])
+        else:
+            ts(out, in_, scale, A.mult)
+
+    def ts(out, in_, s1, o1, s2=None, o2=None):
+        reads = [in_] + [s for s in (s1, s2) if isinstance(s, tuple)]
+        a1 = s1[0] if isinstance(s1, tuple) else s1
+        a2 = s2[0] if isinstance(s2, tuple) else s2
+        if o2 is None:
+            op("v", lambda e: e.tensor_scalar(out[0], in_[0], a1, None, o1), reads, [out])
+        else:
+            op("v", lambda e: e.tensor_scalar(out[0], in_[0], a1, a2, o1, o2), reads, [out])
+
+    def tt(out, a, b, o):
+        op("v", lambda e: e.tensor_tensor(out[0], a[0], b[0], o), [a, b], [out])
+
+    def scan(out, a, b):
+        op("v", lambda e: e.tensor_tensor_scan(out[0], a[0], b[0], 0.0, A.mult, A.add), [a, b], [out])
+
+    def turn(out, in_):
+        op("v", lambda e: e.transpose(out[0], in_[0]), [in_], [out])
+
+    def gather(q, out, win, off):
+        src = win[0].indirect(off[0])
+        if q == "s":
+            op(q, lambda e: e.activation(out[0], src, ACT.Copy), [win, off], [out])
+        else:
+            op(q, lambda e: e.tensor_copy(out[0], src), [win, off], [out])
+
+    def quant(c, s, tile, c0, c1, t0):
+        qc, qs, x = view(c, c0, c1), view(s, c0, c1), view(tile, t0, t0 + 4 * (c1 - c0))
+        op("v", lambda e: e.quantize_mx(qc[0], qs[0], x[0]), [x], [qc, qs])
+
+    bank = [0]
+
+    def product(pairs, rhs, c0, c1):
+        out = view("pb%d" % (bank[0] % 8), 0, c1 - c0)
+        bank[0] += 1
+        rc, rs = view(rhs[0], c0, c1), view(rhs[1], c0, c1)
+        for i, (c, s, a) in enumerate(pairs):
+            lc, ls = view(c, a, a + 128), view(s, a, a + 128)
+            first, last = i == 0, i == len(pairs) - 1
+            op("t", lambda e: e.matmul_mx(out[0], lc[0], ls[0], rc[0], rs[0], first, last), [lc, ls, rc, rs], [out])
+        return out
+
+    for t in range(ROUNDS):
+        for h, (c0, c1) in enumerate(PARTS):
+            for name in ("Ac%d" % t, "As%d" % t):
+                lands(name, c0, c1, "q%d%d" % (t, h if t else 0), 2 * n_in)
+        lands("LR%d" % t, 0, 12, "l%d" % t, n_in)
+
+    load("y", "NX", T.nx[:])
+    load("s", "X", T.x[:, 0:4 * NO], 0, 4 * NO)
+    load("y", "X", T.x[:, 4 * NO:4 * C], 4 * NO, 4 * C)
+    load("s", "UB", T.u[:])
+    load("y", "ALI", T.al[:])
+    load("y", "Wc", T.wc[:])
+    load("s", "Ws", T.ws[:])
+    load("y", "VB", T.v[:])
+
+    def iota(out, pattern, base, mult, loose=False):
+        if loose:
+            op("g", lambda e: e.iota(out[0], pattern, base, mult, allow_small_or_imprecise_dtypes=True), [], [out])
+        else:
+            op("g", lambda e: e.iota(out[0], pattern, base, mult), [], [out])
+    iota(w("PI"), [[1, 1]], 0, 1)
+    for b in range(2):
+        iota(w("AT", 24 * b, 24 * b + 24), [[128, 3], [0, 2], [1, 4]], 0, 0, True)
+    iota(w("LP"), [[16, 8]], 0, 0)
+    iota(w("CT"), [[0, 2048]], 0, 0, True)
+    for b in range(4):
+        d = view("CT", 512 * b + b, 512 * b + 512, 4)
+        op("g", lambda e: e.affine_select(d[0], d[0], [[-1, 128]], A.not_equal, 64.0, 0, 1), [d], [d])
+    fill(w("TAB"), 0.0)
+    ts(w("P31"), w("PI"), 31, A.bitwise_and)
+    ts(w("PHF"), w("P31"), 4.0, A.mult)
+    for name in ("YE", "YO", "RO", "RR", "EO", "ER", "SUM", "OAF"):
+        copy("s", w(name), w("TAB", 0, T[name].shape[1]))
+    copy("s", w("D0", 0, 768, 2), w("TAB", 0, 384))
+    act(w("GG"), w("TAB", 0, 16 * NCH), ACT.Identity, 1.0, 1.0)
+    copy("s", w("GG", 0, 16 * NCH, 8), w("TAB", 0, 2 * NCH))
+    ts(w("AT"), w("AT"), w("PHF"), A.add)
+    for e in range(4):
+        fill(w("WE", e, 192, 4), 2.0 ** (-9 - e))
+        fill(w("WO", e, 192, 4), 2.0 ** (9 - Q2[e]))
+    ts(w("P15"), w("PI"), 15, A.bitwise_and)
+    ts(w("PU"), w("PI"), 4, A.logical_shift_right, 1, A.bitwise_and)
+    ts(w("E3"), w("P15"), EDGE_ROWS[0], A.is_equal)
+    ts(w("E4"), w("P15"), EDGE_ROWS[1], A.is_equal, 17, A.mult)
+    copy("v", w("PUF"), w("PU"))
+    tt(w("LP", 0, 1), w("E3"), w("E4"), A.add)
+    ts(w("PLF"), w("PUF"), -1.0, A.mult, 1.0, A.add)
+    copy("v", w("LPU"), w("LP"))
+    for k in range(1, 4):
+        lo, up = 2.0 ** (EVEN0 + k), 2.0 ** (ODD0 + Q2[k])
+        ts(w("KC", k, k + 1), w("PUF"), up - lo, A.mult, lo, A.add)
+
+    ts(w("CI"), w("NX"), 9, A.logical_shift_right)
+    ts(w("U4"), w("CI"), 4.0, A.mult, -8.0, A.add)
+    tt(w("UU"), w("CI"), w("U4"), A.max)
+    turn(w("UT"), w("UU"))
+    act(w("V2"), w("UT"), ACT.Square)
+    act(w("V4"), w("V2"), ACT.Square)
+    ts(w("NI"), w("NX"), 511, A.bitwise_and)
+    tt(w("PO0"), w("UT"), w("WO"), A.mult)
+    turn(w("NT"), w("NI"))
+    tt(w("PO1"), w("PO0", 0, 192, 2), w("PO0", 1, 192, 2), A.add)
+    for e in range(3):
+        tt(w("ND", e, 192, 4), w("NT", e, 192, 4), w("NT", e + 1, 192, 4), A.subtract)
+    tt(w("ND", 3, 192, 4), w("NT", 3, 192, 4), w("AT"), A.subtract)
+    tt(w("YO", 0, 192, 4), w("PO1", 0, 96, 2), w("PO1", 1, 96, 2), A.add)
+    turn(w("NF"), w("ND"))
+    turn(w("FD"), w("YO"))
+    ts(w("V3"), w("V4"), 3.0, A.mult, -4096.0, A.add)
+    tt(w("NF", 96, 192), w("NF", 96, 192), w("NF", 0, 96), A.subtract)
+    tt(w("FD", 96, 192), w("FD", 96, 192), w("FD", 0, 96), A.subtract)
+    tt(w("VV"), w("V4"), w("V3"), A.max)
+    tt(w("PE0"), w("VV"), w("WE"), A.mult)
+    tt(w("PE1"), w("PE0", 0, 192, 2), w("PE0", 1, 192, 2), A.add)
+    tt(w("YE", 0, 192, 4), w("PE1", 0, 96, 2), w("PE1", 1, 96, 2), A.add)
+    turn(w("FE"), w("YE"))
+    tt(w("FE", 96, 192), w("FE", 96, 192), w("FE", 0, 96), A.subtract)
+
+    def to_row(q, name, e, r):
+        dma(q, T.TAB[r:128:16, :], T[name][e:128:4, :], [(name, 0, 128, 0, 192, 1), ("TAB", 16, 128, 0, 768, 1)], [("TAB", r, r + 1, 0, 768, 1)])
+    for e in range(4):
+        to_row("ysys"[e], "NF", e, 1 + 2 * e)
+    to_row("s", "FD", 0, 2)
+    to_row("y", "FE", 0, 0)
+
+    def send_x(t, c0, c1, h):
+        for a, b in (("Qc%d", "Ac%d"), ("Qs%d", "As%d")):
+            s, d = T[a % t][:, c0:c1], T[b % t][:, c0:c1]
+            if a == "Qc%d":
+                s, d = s.bitcast(dt.uint8), d.bitcast(dt.uint8)
+            send(d, s, (a % t, 0, 128, c0, c1, 1), "q%d%d" % (t, h))
+
+    def quant_x(t, h):
+        c0, c1 = PARTS[h]
+        quant("Qc%d" % t, "Qs%d" % t, "X", c0, c1, 4 * c0)
+
+    quant_x(0, 0)
+    quant_x(0, 1)
+    send_x(0, 0, C, 0)
+    quant("Uc", "Us", "UB", 0, 128, 0)
+    op("v", lambda e: e.tensor_copy(T.Pc[:, 0:128].bitcast(dt.uint32), T.Uc[:, 0:128].bitcast(dt.uint32).indirect(T.LPU[:, 0:8])), [w("Uc"), w("LPU")], [w("Pc")])
+    op("v", lambda e: e.tensor_copy(T.Ps[:, 0:128], T.Us[:, 0:128].indirect(T.LPU[:, 0:8])), [w("Us"), w("LPU")], [w("Ps")])
+    for o, a, b in ((0, 0, 14), (14, 0, 2), (16, 14, 24), (26, 14, 16)):
+        copy("v", w("AL0", o, o + b - a), w("ALI", a, b))
+    ts(w("L2O", 0, 16), w("AL0", 0, 16), 2.0, A.mult)
+    ts(w("L2R", 0, 12), w("AL0", 16, 28), 2.0, A.mult)
+    quant("CTc", "CTs", "CT", 0, 512, 0)
+
+    def score(t, h):
+        c0, c1 = PARTS[h]
+        return product([("Pc", "Ps", 0)], ("Qc%d" % t, "Qs%d" % t), c0, c1)
+
+    def unpack(src, dst, h, qs):
+        c0, c1 = PARTS[h]
+        outs = [product([("CTc", "CTs", 128 * b)], src, c0, c1) for b in range(4)]
+        return [(qs[b], w(dst, C * b + c0, C * b + c1), outs[b]) for b in range(4)]
+
+    def take(jobs):
+        for q, out, ps in jobs:
+            copy(q, out, ps, 2.0 ** -6)
+
+    def bits(ps, h):
+        c0, c1 = PARTS[h]
+        ts(w("D1", 2 * c0, 2 * c1, 2), ps, 0.0, A.is_gt)
+
+    def choose(h):
+        c0, c1 = PARTS[h]
+        scan(w("TW", 7 + 2 * c0, 7 + 2 * c1), w("D0", 2 * c0, 2 * c1), w("D1", 2 * c0, 2 * c1))
+
+    def edges(h):
+        c0, c1 = PARTS[h]
+        m, name = c1 - c0, ("EO", "ER")[h]
+        for a, b, o in ((0, m, 0), (0, 16, m)):
+            copy("s", view(name, o, o + b - a, 1, 0, 32), view("D1", 2 * (c0 + a), 2 * (c0 + b), 2, 0, 32))
+
+    def turns(h, src, dst, p1):
+        m = (14, 10)[h]
+        first, second = ((0, 14), (8, 22))[h]
+        turn(view(dst, 32 * first, 32 * first + 16 * (m + 2), 1, 0, p1), view(src, 0, 16 * (m + 2), 1, 0, p1))
+        turn(view(dst, 32 * second, 32 * second + 32, 1, 0, p1), view(src, 16 * (m - 1), 16 * (m + 1), 1, 0, p1))
+        turn(view(dst, 32 * second + 32, 32 * second + 32 + 16 * m, 1, 0, p1), view(src, 16, 16 * (m + 1), 1, 0, p1))
+
+    def carries(t):
+        n2 = 2 * NCH
+        p = lambda name, a, b, step, q: view(name, a, b, step, 32 * q, 32 * q + 32)
+        tt(p("MM", 0, n2, 2, 0), p("MA", 0, NCH, 1, 0), p("MB", 0, NCH, 1, 0), A.mult)
+        masks = (sum(2 ** (ODD0 + k) for k in Q2), sum(2 ** (EVEN0 + k) for k in range(4)))
+        for s in range(7):
+            q, o = s // 2, s % 2
+            q2, o2 = (s + 1) // 2, (s + 1) % 2
+            tt(p("YY", 0, NCH, 1, q), p("CH", (0, 18)[o], 32 * NCH, 32, q), p("MM", o, n2, 2, q), A.mult)
+            ts(p("MM", o2, n2, 2, q2), p("YY", 0, NCH, 1, q), masks[o], A.bitwise_and)
+        for k in range(1, 4):
+            ts(w("GG", k, 16 * NCH, 8), w("MM"), w("KC", k, k + 1), A.is_lt)
+        ts(w("GG", 4, 16 * NCH, 16), w("MM", 0, n2, 2), 0.0, A.is_gt, w("PLF"), A.mult)
+        ts(w("GG", 12, 16 * NCH, 16), w("MM", 1, n2, 2), 0.0, A.is_gt, w("PUF"), A.mult)
+        scan(w("XS"), w("GG"), w("CH", 1, 32 * NCH, 2))
+        tt(w("SUM", 0, 28, 2), w("XS", 7, 224, 16), w("XS", 239, 448, 16), A.add)
+        tt(w("SUM", 1, 27, 2), w("XS", 247, 448, 16), w("XS", 15, 216, 16), A.add)
+        new = "AL%d" % (t + 1)
+        tt(w(new), w("SUM"), w("AL%d" % t), A.add)
+        copy("v", w("LS%d" % t), w(new, 16, 28))
+        send(T["LR%d" % t][:], T["LS%d" % t][:], ("LS%d" % t, 0, 128, 0, 12, 1), "l%d" % t)
+        copy("v", w("LO%d" % t), w(new, 0, 16))
+
+    def layer(h, bs=range(4)):
+        z = (("ZOc", "ZOs"), ("ZRc", "ZRs"))[h]
+        m = (NO, NR)[h]
+        return [product([("Wc", "Ws", 128 * b), ("CTc", "CTs", 128 * b)], z, 0, m) for b in bs]
+
+    def state(h, outs, qs, bs=range(4)):
+        c0, c1 = PARTS[h]
+        for b in bs:
+            copy(qs[b], w("X", 4 * c0 + b, 4 * c1, 4), outs[b], 2.0 ** -6)
+
+    def addresses_out():
+        copy("v", w("OAF", 0, 14), w("AL%d" % ROUNDS, 0, 14))
+        copy("v", w("OAF", 14, 24), w("LR%d" % (ROUNDS - 1), 0, 10))
+        turn(w("OAT"), w("OAF"))
+        for k in range(8):
+            p0 = 32 * (k // 2)
+            dma("y", T.oa[k:k + 1, :], T.OAT[p0:p0 + 24, 16 * (k % 2):16 * (k % 2) + 16], [("OAT", p0, p0 + 24, 0, 32, 1)])
+
+    sa = score(0, 0)
+    sb = score(0, 1)
+    for t in range(ROUNDS):
+        last = t + 1 == ROUNDS
+        fa = unpack(("Qc%d" % t, "Qs%d" % t), "FO", 0, "ssss")
+        if t == 0:
+            bits(sa, 0)
+            edges(0)
+            take(fa)
+            bits(sb, 1)
+            edges(1)
+            for ph in range(4):
+                copy("sv"[ph % 2], w("D1", 2 * ph + 1, 768, 8), w("TAB", 192 * ph, 192 * ph + 96))
+                copy("vs"[ph % 2], w("D0", 2 * ph + 1, 768, 8), w("TAB", 192 * ph + 96, 192 * ph + 192))
+            choose(0)
+            turns(0, "EO", "CE", 32)
+        else:
+            bits(sb, 1)
+            edges(1)
+        choose(1)
+        gather("v", w("RO", 0, 240), w("TW", 8, 776), w("L2O", 0, 15))
+        gather("s", w("RR", 0, 176), w("TW", 8, 776), w("L2R", 0, 11))
+        turns(1, "ER", "CE", 32)
+        act(view("MA", 0, NCH, 1, 0, 32), view("CE", EDGE_ROWS[0], 32 * NCH, 32, 0, 32), ACT.Identity, 3.0 * 2.0 ** EVEN0, 2.0 ** EVEN0)
+        act(view("MB", 0, NCH, 1, 0, 32), view("CE", EDGE_ROWS[1], 32 * NCH, 32, 0, 32), ACT.Identity, 1.0, 1.0)
+        turns(0, "RO", "CH", 128)
+        turns(1, "RR", "CH", 128)
+        if t:
+            take(fa)
+        take(unpack(("Qc%d" % t, "Qs%d" % t), "FO", 1, "ssss"))
+        carries(t)
+        take(unpack(("Ac%d" % t, "As%d" % t), "FP", 0, "ssss"))
+        for b in range(4):
+            gather("vsvs"[b], w("ZO", b, 4 * NO, 4), w("FO", C * b, C * b + C), w("LO%d" % t, 0, 14))
+        quant("ZOc", "ZOs", "ZO", 0, NO, 0)
+        take(unpack(("Ac%d" % t, "As%d" % t), "FP", 1, "vsvs"))
+        outs = layer(0)
+        if t == 0:
+            quant("Vc", "Vs", "VB", 0, 128, 0)
+        if not last:
+            ts(w("L2O", 0, 16), w("AL%d" % (t + 1), 0, 16), 2.0, A.mult)
+        for b in range(4):
+            gather("vsvs"[b], w("ZR", b, 4 * NR, 4), w("FP", C * b, C * b + C), w("LR%d" % t, 0, 10))
+        quant("ZRc", "ZRs", "ZR", 0, NR, 0)
+        outs2 = layer(1, (0, 1))
+        if last:
+            addresses_out()
+        state(0, outs, "svsv")
+        quant_x(t + 1, 0)
+        if not last:
+            send_x(t + 1, 0, NO, 0)
+            sa = score(t + 1, 0)
+            copy("v", w("AL%d" % (t + 1), 16, 28), w("LR%d" % t))
+            ts(w("L2R", 0, 12), w("LR%d" % t), 2.0, A.mult)
+        outs2 += layer(1, (2, 3))
+        if last:
+            state(1, outs2, "svsv")
+        else:
+            state(1, outs2, "svss", (0, 1))
+            bits(sa, 0)
+            edges(0)
+            choose(0)
+            state(1, outs2, "svss", (2, 3))
+            turns(0, "EO", "CE", 32)
+        quant_x(t + 1, 1)
+        if not last:
+            send_x(t + 1, NO, C, 1)
+            sb = score(t + 1, 1)
+
+    qc, qs = "Qc%d" % ROUNDS, "Qs%d" % ROUNDS
+    for h, (c0, c1) in enumerate(PARTS):
+        out = product([("Vc", "Vs", 0)], (qc, qs), c0, c1)
+        dma("ys"[h], T.oc[:, 4 * c0:4 * c1], T[qc][:, c0:c1].bitcast(dt.uint8), [(qc, 0, 128, c0, c1, 1)])
+        copy("sv"[h], w("Y", c0, c1), out)
+        dma("ys"[h], T.y[:, c0:c1], T.Y[:, c0:c1], [("Y", 0, 128, c0, c1, 1)])
+    for k in range(4):
+        dma("ys"[k % 2], T.osc[4 * k:4 * k + 4, :], T[qs][32 * k:32 * k + 4, :], [(qs, 0, 128, 0, C, 1)])
+
+    for s in sorted(count):
+        if need_end.get(s, 0) < count[s]:
+            g.wait_ge(T.sem[s], count[s])

@@ -3,9 +3,10 @@ from concourse.mybir import dt, AluOpType, ActivationFunctionType
 CODES = "float8_e4m3fn_x4"
 C, NO, NR, ROUNDS = 384, 224, 160, 3
 PARTS = ((0, NO), (NO, C))
-Q2 = (0, 4, 8, 13)
-EVEN0, ODD0 = 13, 4
+Q2 = (0, 4, 8, 12)
+EVEN0, ODD0 = 15, 3
 NCH = 28
+A_ROW = 9
 EDGE_ROWS = (4, 6)
 
 _F = "float32"
@@ -13,17 +14,16 @@ SCRATCH = {
     "NX": ("sbuf", [128, 192], "int32"), "CI": ("sbuf", [128, 192], "int32"), "NI": ("sbuf", [128, 192], "int32"),
     "NT": ("sbuf", [128, 192], "int32"), "ND": ("sbuf", [128, 192], _F), "AT": ("sbuf", [128, 48], _F), "NF": ("sbuf", [128, 192], _F),
     "U4": ("sbuf", [128, 192], _F), "UU": ("sbuf", [128, 192], _F), "UT": ("sbuf", [128, 192], _F), "V2": ("sbuf", [128, 192], _F),
-    "V4": ("sbuf", [128, 192], _F), "V3": ("sbuf", [128, 192], _F), "VV": ("sbuf", [128, 192], _F),
-    "PE0": ("sbuf", [128, 192], _F), "PO0": ("sbuf", [128, 192], _F), "PE1": ("sbuf", [128, 96], _F), "PO1": ("sbuf", [128, 96], _F),
-    "YE": ("sbuf", [128, 192], _F), "YO": ("sbuf", [128, 192], _F), "FE": ("sbuf", [128, 192], _F), "FD": ("sbuf", [128, 192], _F),
-    "WE": ("sbuf", [128, 192], _F), "WO": ("sbuf", [128, 192], _F),
+    "V4": ("sbuf", [128, 192], _F), "SE": ("sbuf", [128, 192], _F), "SO": ("sbuf", [128, 192], _F), "FE": ("sbuf", [128, 192], _F),
+    "FD": ("sbuf", [128, 192], _F), "HE": ("sbuf", [128, 192], _F), "HO": ("sbuf", [128, 192], _F),
+    "ZZ": ("sbuf", [128, 16 * NCH], _F), "AW": ("sbuf", [128, C], _F), "M9": ("sbuf", [128, 1], _F), "SC": ("sbuf", [128, 1], _F),
     "TAB": ("sbuf", [128, 768], _F), "D0": ("sbuf", [128, 768], _F), "D1": ("sbuf", [128, 768], _F),
     "TW": ("sbuf", [128, 776], _F), "RO": ("sbuf", [128, 256], _F), "RR": ("sbuf", [128, 192], _F),
     "EO": ("sbuf", [128, 256], "bfloat16"), "ER": ("sbuf", [128, 192], "bfloat16"),
     "CH": ("sbuf", [128, 32 * NCH], _F), "CE": ("sbuf", [128, 32 * NCH], "bfloat16"),
     "MA": ("sbuf", [128, NCH], _F), "MB": ("sbuf", [128, NCH], _F),
     "MM": ("sbuf", [128, 2 * NCH], "int32"), "YY": ("sbuf", [128, NCH], "int32"),
-    "GG": ("sbuf", [128, 16 * NCH], _F), "XS": ("sbuf", [128, 16 * NCH], _F), "SUM": ("sbuf", [128, NCH], _F),
+    "GG": ("sbuf", [128, 16 * NCH], _F), "XS": ("sbuf", [128, 16 * NCH], _F),
     "PI": ("sbuf", [128, 1], "int32"), "P15": ("sbuf", [128, 1], "int32"), "PU": ("sbuf", [128, 1], "int32"),
     "P31": ("sbuf", [128, 1], "int32"), "PUF": ("sbuf", [128, 1], _F), "PLF": ("sbuf", [128, 1], _F), "PHF": ("sbuf", [128, 1], _F),
     "E3": ("sbuf", [128, 1], "int32"), "E4": ("sbuf", [128, 1], "int32"), "KC": ("sbuf", [128, 4], _F),
@@ -44,8 +44,8 @@ SCRATCH = {
 for _t in range(ROUNDS + 1):
     SCRATCH["Qc%d" % _t] = ("sbuf", [128, C], CODES)
     SCRATCH["Qs%d" % _t] = ("sbuf", [128, C], "uint8")
-    SCRATCH["AL%d" % _t] = ("sbuf", [128, NCH], _F)
 for _t in range(ROUNDS):
+    SCRATCH["AL%d" % _t] = ("sbuf", [128, NCH], _F)
     SCRATCH["Ac%d" % _t] = ("sbuf", [128, C], CODES)
     SCRATCH["As%d" % _t] = ("sbuf", [128, C], "uint8")
     SCRATCH["LO%d" % _t] = ("sbuf", [128, 16], "uint16")
@@ -150,7 +150,8 @@ def rank_program(g, core, T, topo):
         op("v", lambda e: e.memset(ap[0], val), [], [ap])
 
     def act(out, in_, func=ACT.Copy, scale=1.0, bias=0.0):
-        op("s", lambda e: e.activation(out[0], in_[0], func, bias=bias, scale=scale), [in_], [out])
+        a = scale[0] if isinstance(scale, tuple) else scale
+        op("s", lambda e: e.activation(out[0], in_[0], func, bias=bias, scale=a), [in_] + ([scale] if isinstance(scale, tuple) else []), [out])
 
     def copy(q, out, in_, scale=None):
         if q == "s":
@@ -225,26 +226,31 @@ def rank_program(g, core, T, topo):
     for b in range(2):
         iota(w("AT", 24 * b, 24 * b + 24), [[128, 3], [0, 2], [1, 4]], 0, 0, True)
     iota(w("LP"), [[16, 8]], 0, 0)
+    iota(w("AW"), [[1, C]], 0, 0, True)
     iota(w("CT"), [[0, 2048]], 0, 0, True)
     for b in range(4):
         d = view("CT", 512 * b + b, 512 * b + 512, 4)
         op("g", lambda e: e.affine_select(d[0], d[0], [[-1, 128]], A.not_equal, 64.0, 0, 1), [d], [d])
-    fill(w("TAB"), 0.0)
-    ts(w("P31"), w("PI"), 31, A.bitwise_and)
-    ts(w("PHF"), w("P31"), 4.0, A.mult)
-    for name in ("YE", "YO", "RO", "RR", "EO", "ER", "SUM", "OAF"):
-        copy("s", w(name), w("TAB", 0, T[name].shape[1]))
-    copy("s", w("D0", 0, 768, 2), w("TAB", 0, 384))
-    act(w("GG"), w("TAB", 0, 16 * NCH), ACT.Identity, 1.0, 1.0)
-    copy("s", w("GG", 0, 16 * NCH, 8), w("TAB", 0, 2 * NCH))
-    ts(w("AT"), w("AT"), w("PHF"), A.add)
-    for e in range(4):
-        fill(w("WE", e, 192, 4), 2.0 ** (-9 - e))
-        fill(w("WO", e, 192, 4), 2.0 ** (9 - Q2[e]))
+    fill(w("ZZ"), 0.0)
     ts(w("P15"), w("PI"), 15, A.bitwise_and)
+    ts(w("P31"), w("PI"), 31, A.bitwise_and)
+    ts(w("M9"), w("P15"), A_ROW, A.is_equal)
+    ts(w("PHF"), w("P31"), 4.0, A.mult)
+    for ph in range(4):
+        act(w("TAB", 192 * ph, 192 * ph + 96), w("AW", ph, C, 4), ACT.Copy, w("M9"))
+        copy("s", w("TAB", 192 * ph + 96, 192 * ph + 192), w("ZZ", 0, 96))
+    copy("s", w("D0", 0, 768, 2), w("ZZ", 0, 384))
+    for name in ("RO", "RR", "EO", "ER", "OAF"):
+        copy("s", w(name), w("ZZ", 0, T[name].shape[1]))
+    ts(w("AT"), w("AT"), w("PHF"), A.add)
+    for name, ratio in (("HE", 2.0), ("HO", 16.0)):
+        fill(w(name), ratio)
+        fill(w(name, 0, 192, 4), 0.0)
+    ts(w("SC"), w("P15"), 0, A.is_equal, 2.0 ** (ODD0 - EVEN0 - 3) - 1.0, A.mult)
     ts(w("PU"), w("PI"), 4, A.logical_shift_right, 1, A.bitwise_and)
     ts(w("E3"), w("P15"), EDGE_ROWS[0], A.is_equal)
     ts(w("E4"), w("P15"), EDGE_ROWS[1], A.is_equal, 17, A.mult)
+    ts(w("SC"), w("SC"), 1.0, A.add)
     copy("v", w("PUF"), w("PU"))
     tt(w("LP", 0, 1), w("E3"), w("E4"), A.add)
     ts(w("PLF"), w("PUF"), -1.0, A.mult, 1.0, A.add)
@@ -259,32 +265,30 @@ def rank_program(g, core, T, topo):
     turn(w("UT"), w("UU"))
     act(w("V2"), w("UT"), ACT.Square)
     act(w("V4"), w("V2"), ACT.Square)
+    scan(w("SO"), w("HO"), w("UT"))
     ts(w("NI"), w("NX"), 511, A.bitwise_and)
-    tt(w("PO0"), w("UT"), w("WO"), A.mult)
+    turn(w("FD"), w("SO"))
     turn(w("NT"), w("NI"))
-    tt(w("PO1"), w("PO0", 0, 192, 2), w("PO0", 1, 192, 2), A.add)
+    scan(w("SE"), w("HE"), w("V4"))
+    tt(w("FD", 96, 192), w("FD", 96, 192), w("FD", 0, 96), A.subtract)
+    turn(w("FE"), w("SE"))
     for e in range(3):
         tt(w("ND", e, 192, 4), w("NT", e, 192, 4), w("NT", e + 1, 192, 4), A.subtract)
     tt(w("ND", 3, 192, 4), w("NT", 3, 192, 4), w("AT"), A.subtract)
-    tt(w("YO", 0, 192, 4), w("PO1", 0, 96, 2), w("PO1", 1, 96, 2), A.add)
-    turn(w("NF"), w("ND"))
-    turn(w("FD"), w("YO"))
-    ts(w("V3"), w("V4"), 3.0, A.mult, -4096.0, A.add)
-    tt(w("NF", 96, 192), w("NF", 96, 192), w("NF", 0, 96), A.subtract)
-    tt(w("FD", 96, 192), w("FD", 96, 192), w("FD", 0, 96), A.subtract)
-    tt(w("VV"), w("V4"), w("V3"), A.max)
-    tt(w("PE0"), w("VV"), w("WE"), A.mult)
-    tt(w("PE1"), w("PE0", 0, 192, 2), w("PE0", 1, 192, 2), A.add)
-    tt(w("YE", 0, 192, 4), w("PE1", 0, 96, 2), w("PE1", 1, 96, 2), A.add)
-    turn(w("FE"), w("YE"))
     tt(w("FE", 96, 192), w("FE", 96, 192), w("FE", 0, 96), A.subtract)
+    turn(w("NF"), w("ND"))
+    tt(w("NF", 96, 192), w("NF", 96, 192), w("NF", 0, 96), A.subtract)
 
     def to_row(q, name, e, r):
         dma(q, T.TAB[r:128:16, :], T[name][e:128:4, :], [(name, 0, 128, 0, 192, 1), ("TAB", 16, 128, 0, 768, 1)], [("TAB", r, r + 1, 0, 768, 1)])
+    to_row("s", "FD", 3, 2)
+    to_row("y", "FE", 3, 0)
     for e in range(4):
-        to_row("ysys"[e], "NF", e, 1 + 2 * e)
-    to_row("s", "FD", 0, 2)
-    to_row("y", "FE", 0, 0)
+        to_row("sysy"[e], "NF", e, 1 + 2 * e)
+    act(w("GG"), w("ZZ"), ACT.Identity, 1.0, 1.0)
+    copy("s", w("GG", 0, 16 * NCH, 8), w("ZZ", 0, 2 * NCH))
+    for t in range(ROUNDS):
+        copy("s", w("AL%d" % t, 27, 28), w("ZZ", 0, 1))
 
     def send_x(t, c0, c1, h):
         for a, b in (("Qc%d", "Ac%d"), ("Qs%d", "As%d")):
@@ -303,10 +307,10 @@ def rank_program(g, core, T, topo):
     quant("Uc", "Us", "UB", 0, 128, 0)
     op("v", lambda e: e.tensor_copy(T.Pc[:, 0:128].bitcast(dt.uint32), T.Uc[:, 0:128].bitcast(dt.uint32).indirect(T.LPU[:, 0:8])), [w("Uc"), w("LPU")], [w("Pc")])
     op("v", lambda e: e.tensor_copy(T.Ps[:, 0:128], T.Us[:, 0:128].indirect(T.LPU[:, 0:8])), [w("Us"), w("LPU")], [w("Ps")])
-    for o, a, b in ((0, 0, 14), (14, 0, 2), (16, 14, 24), (26, 14, 16)):
-        copy("v", w("AL0", o, o + b - a), w("ALI", a, b))
-    ts(w("L2O", 0, 16), w("AL0", 0, 16), 2.0, A.mult)
-    ts(w("L2R", 0, 12), w("AL0", 16, 28), 2.0, A.mult)
+    for name, o, a, b in (("L2O", 0, 0, 14), ("L2O", 14, 0, 2), ("L2R", 0, 14, 24), ("L2R", 10, 14, 16)):
+        ts(w(name, o, o + b - a), w("ALI", a, b), 2.0, A.mult)
+    ts(w("GG", 5, 16 * NCH, 16), w("ZZ", 0, NCH), w("PLF"), A.add)
+    ts(w("GG", 13, 16 * NCH, 16), w("ZZ", 0, NCH), w("PUF"), A.add)
     quant("CTc", "CTs", "CT", 0, 512, 0)
 
     def score(t, h):
@@ -343,10 +347,14 @@ def rank_program(g, core, T, topo):
         turn(view(dst, 32 * second, 32 * second + 32, 1, 0, p1), view(src, 16 * (m - 1), 16 * (m + 1), 1, 0, p1))
         turn(view(dst, 32 * second + 32, 32 * second + 32 + 16 * m, 1, 0, p1), view(src, 16, 16 * (m + 1), 1, 0, p1))
 
+    def start():
+        p = lambda name, a, b, step: view(name, a, b, step, 0, 32)
+        act(p("MA", 0, NCH, 1), p("CE", EDGE_ROWS[0], 32 * NCH, 32), ACT.Identity, 3.0 * 2.0 ** EVEN0, 2.0 ** EVEN0)
+        act(p("MB", 0, NCH, 1), p("CE", EDGE_ROWS[1], 32 * NCH, 32), ACT.Identity, 1.0, 1.0)
+
     def carries(t):
         n2 = 2 * NCH
         p = lambda name, a, b, step, q: view(name, a, b, step, 32 * q, 32 * q + 32)
-        tt(p("MM", 0, n2, 2, 0), p("MA", 0, NCH, 1, 0), p("MB", 0, NCH, 1, 0), A.mult)
         masks = (sum(2 ** (ODD0 + k) for k in Q2), sum(2 ** (EVEN0 + k) for k in range(4)))
         for s in range(7):
             q, o = s // 2, s % 2
@@ -355,13 +363,11 @@ def rank_program(g, core, T, topo):
             ts(p("MM", o2, n2, 2, q2), p("YY", 0, NCH, 1, q), masks[o], A.bitwise_and)
         for k in range(1, 4):
             ts(w("GG", k, 16 * NCH, 8), w("MM"), w("KC", k, k + 1), A.is_lt)
-        ts(w("GG", 4, 16 * NCH, 16), w("MM", 0, n2, 2), 0.0, A.is_gt, w("PLF"), A.mult)
-        ts(w("GG", 12, 16 * NCH, 16), w("MM", 1, n2, 2), 0.0, A.is_gt, w("PUF"), A.mult)
+        ts(w("GG", 4, 16 * NCH, 8), w("MM"), 0.0, A.is_gt)
         scan(w("XS"), w("GG"), w("CH", 1, 32 * NCH, 2))
-        tt(w("SUM", 0, 28, 2), w("XS", 7, 224, 16), w("XS", 239, 448, 16), A.add)
-        tt(w("SUM", 1, 27, 2), w("XS", 247, 448, 16), w("XS", 15, 216, 16), A.add)
-        new = "AL%d" % (t + 1)
-        tt(w(new), w("SUM"), w("AL%d" % t), A.add)
+        new = "AL%d" % t
+        tt(w(new, 0, 28, 2), w("XS", 7, 224, 16), w("XS", 239, 448, 16), A.add)
+        tt(w(new, 1, 27, 2), w("XS", 247, 448, 16), w("XS", 15, 216, 16), A.add)
         copy("v", w("LS%d" % t), w(new, 16, 28))
         send(T["LR%d" % t][:], T["LS%d" % t][:], ("LS%d" % t, 0, 128, 0, 12, 1), "l%d" % t)
         copy("v", w("LO%d" % t), w(new, 0, 16))
@@ -377,7 +383,7 @@ def rank_program(g, core, T, topo):
             copy(qs[b], w("X", 4 * c0 + b, 4 * c1, 4), outs[b], 2.0 ** -6)
 
     def addresses_out():
-        copy("v", w("OAF", 0, 14), w("AL%d" % ROUNDS, 0, 14))
+        copy("v", w("OAF", 0, 14), w("AL%d" % (ROUNDS - 1), 0, 14))
         copy("v", w("OAF", 14, 24), w("LR%d" % (ROUNDS - 1), 0, 10))
         turn(w("OAT"), w("OAF"))
         for k in range(8):
@@ -392,27 +398,25 @@ def rank_program(g, core, T, topo):
         if t == 0:
             bits(sa, 0)
             edges(0)
-            take(fa)
             bits(sb, 1)
             edges(1)
             for ph in range(4):
-                copy("sv"[ph % 2], w("D1", 2 * ph + 1, 768, 8), w("TAB", 192 * ph, 192 * ph + 96))
-                copy("vs"[ph % 2], w("D0", 2 * ph + 1, 768, 8), w("TAB", 192 * ph + 96, 192 * ph + 192))
+                copy("sv"[ph % 2], w("D1", 2 * ph + 1, 768, 8), w("TAB", 192 * ph, 192 * ph + 96), w("SC"))
+                copy("vs"[ph % 2], w("D0", 2 * ph + 1, 768, 8), w("TAB", 192 * ph + 96, 192 * ph + 192), w("SC"))
             choose(0)
             turns(0, "EO", "CE", 32)
         else:
             bits(sb, 1)
             edges(1)
         choose(1)
-        gather("v", w("RO", 0, 240), w("TW", 8, 776), w("L2O", 0, 15))
-        gather("s", w("RR", 0, 176), w("TW", 8, 776), w("L2R", 0, 11))
+        gather("s", w("RO", 0, 240), w("TW", 8, 776), w("L2O", 0, 15))
+        gather("v", w("RR", 0, 176), w("TW", 8, 776), w("L2R", 0, 11))
         turns(1, "ER", "CE", 32)
-        act(view("MA", 0, NCH, 1, 0, 32), view("CE", EDGE_ROWS[0], 32 * NCH, 32, 0, 32), ACT.Identity, 3.0 * 2.0 ** EVEN0, 2.0 ** EVEN0)
-        act(view("MB", 0, NCH, 1, 0, 32), view("CE", EDGE_ROWS[1], 32 * NCH, 32, 0, 32), ACT.Identity, 1.0, 1.0)
-        turns(0, "RO", "CH", 128)
+        start()
         turns(1, "RR", "CH", 128)
-        if t:
-            take(fa)
+        tt(view("MM", 0, 2 * NCH, 2, 0, 32), view("MA", 0, NCH, 1, 0, 32), view("MB", 0, NCH, 1, 0, 32), A.mult)
+        turns(0, "RO", "CH", 128)
+        take(fa)
         take(unpack(("Qc%d" % t, "Qs%d" % t), "FO", 1, "ssss"))
         carries(t)
         take(unpack(("Ac%d" % t, "As%d" % t), "FP", 0, "ssss"))
@@ -424,7 +428,7 @@ def rank_program(g, core, T, topo):
         if t == 0:
             quant("Vc", "Vs", "VB", 0, 128, 0)
         if not last:
-            ts(w("L2O", 0, 16), w("AL%d" % (t + 1), 0, 16), 2.0, A.mult)
+            ts(w("L2O", 0, 16), w("AL%d" % t, 0, 16), 2.0, A.mult)
         for b in range(4):
             gather("vsvs"[b], w("ZR", b, 4 * NR, 4), w("FP", C * b, C * b + C), w("LR%d" % t, 0, 10))
         quant("ZRc", "ZRs", "ZR", 0, NR, 0)
@@ -436,7 +440,6 @@ def rank_program(g, core, T, topo):
         if not last:
             send_x(t + 1, 0, NO, 0)
             sa = score(t + 1, 0)
-            copy("v", w("AL%d" % (t + 1), 16, 28), w("LR%d" % t))
             ts(w("L2R", 0, 12), w("LR%d" % t), 2.0, A.mult)
         outs2 += layer(1, (2, 3))
         if last:
@@ -460,7 +463,7 @@ def rank_program(g, core, T, topo):
         copy("sv"[h], w("Y", c0, c1), out)
         dma("ys"[h], T.y[:, c0:c1], T.Y[:, c0:c1], [("Y", 0, 128, c0, c1, 1)])
     for k in range(4):
-        dma("ys"[k % 2], T.osc[4 * k:4 * k + 4, :], T[qs][32 * k:32 * k + 4, :], [(qs, 0, 128, 0, C, 1)])
+        dma("y", T.osc[4 * k:4 * k + 4, :], T[qs][32 * k:32 * k + 4, :], [(qs, 0, 128, 0, C, 1)])
 
     for s in sorted(count):
         if need_end.get(s, 0) < count[s]:

from concourse.mybir import dt, AluOpType, ActivationFunctionType

CODES = "float8_e4m3fn_x4"
C, NO, NR, ROUNDS = 384, 224, 160, 3
PARTS = ((0, NO), (NO, C))
Q2 = (0, 4, 8, 12)
EVEN0, ODD0 = 15, 3
NCH = 28
A_ROW = 9
EDGE_ROWS = (4, 6)

_F = "float32"
SCRATCH = {
    "NX": ("sbuf", [128, 192], "int32"), "CI": ("sbuf", [128, 192], "int32"), "NI": ("sbuf", [128, 192], "int32"),
    "NT": ("sbuf", [128, 192], "int32"), "ND": ("sbuf", [128, 192], _F), "AT": ("sbuf", [128, 48], _F), "NF": ("sbuf", [128, 192], _F),
    "U4": ("sbuf", [128, 192], _F), "UU": ("sbuf", [128, 192], _F), "UT": ("sbuf", [128, 192], _F), "V2": ("sbuf", [128, 192], _F),
    "V4": ("sbuf", [128, 192], _F), "SE": ("sbuf", [128, 192], _F), "SO": ("sbuf", [128, 192], _F), "FE": ("sbuf", [128, 192], _F),
    "FD": ("sbuf", [128, 192], _F), "HE": ("sbuf", [128, 192], _F), "HO": ("sbuf", [128, 192], _F),
    "ZZ": ("sbuf", [128, 16 * NCH], _F), "AW": ("sbuf", [128, C], _F), "M9": ("sbuf", [128, 1], _F), "SC": ("sbuf", [128, 1], _F),
    "TAB": ("sbuf", [128, 768], _F), "D0": ("sbuf", [128, 768], _F), "D1": ("sbuf", [128, 768], _F),
    "TW": ("sbuf", [128, 776], _F), "RO": ("sbuf", [128, 256], _F), "RR": ("sbuf", [128, 192], _F),
    "EO": ("sbuf", [128, 256], "bfloat16"), "ER": ("sbuf", [128, 192], "bfloat16"),
    "CH": ("sbuf", [128, 32 * NCH], _F), "CE": ("sbuf", [128, 32 * NCH], "bfloat16"),
    "MA": ("sbuf", [128, NCH], _F), "MB": ("sbuf", [128, NCH], _F),
    "MM": ("sbuf", [128, 2 * NCH], "int32"), "YY": ("sbuf", [128, NCH], "int32"),
    "GG": ("sbuf", [128, 16 * NCH], _F), "XS": ("sbuf", [128, 16 * NCH], _F),
    "PI": ("sbuf", [128, 1], "int32"), "P15": ("sbuf", [128, 1], "int32"), "PU": ("sbuf", [128, 1], "int32"),
    "P31": ("sbuf", [128, 1], "int32"), "PUF": ("sbuf", [128, 1], _F), "PLF": ("sbuf", [128, 1], _F), "PHF": ("sbuf", [128, 1], _F),
    "E3": ("sbuf", [128, 1], "int32"), "E4": ("sbuf", [128, 1], "int32"), "KC": ("sbuf", [128, 4], _F),
    "LP": ("sbuf", [128, 8], "int32"), "LPU": ("sbuf", [128, 8], "uint16"),
    "ALI": ("sbuf", [128, 24], "int32"), "OAF": ("sbuf", [128, 32], _F), "OAT": ("sbuf", [128, 32], _F),
    "L2O": ("sbuf", [128, 16], "uint16"), "L2R": ("sbuf", [128, 16], "uint16"),
    "CT": ("sbuf", [128, 2048], "bfloat16"), "CTc": ("sbuf", [128, 512], CODES), "CTs": ("sbuf", [128, 512], "uint8"),
    "UB": ("sbuf", [128, 512], "bfloat16"), "Uc": ("sbuf", [128, 128], CODES), "Us": ("sbuf", [128, 128], "uint8"),
    "Pc": ("sbuf", [128, 128], CODES), "Ps": ("sbuf", [128, 128], "uint8"),
    "VB": ("sbuf", [128, 512], "bfloat16"), "Vc": ("sbuf", [128, 128], CODES), "Vs": ("sbuf", [128, 128], "uint8"),
    "Wc": ("sbuf", [128, 512], CODES), "Ws": ("sbuf", [128, 512], "uint8"),
    "X": ("sbuf", [128, 4 * C], "bfloat16"), "FO": ("sbuf", [128, 4 * C], "bfloat16"), "FP": ("sbuf", [128, 4 * C], "bfloat16"),
    "ZO": ("sbuf", [128, 4 * NO], "bfloat16"), "ZR": ("sbuf", [128, 4 * NR], "bfloat16"),
    "ZOc": ("sbuf", [128, NO], CODES), "ZOs": ("sbuf", [128, NO], "uint8"),
    "ZRc": ("sbuf", [128, NR], CODES), "ZRs": ("sbuf", [128, NR], "uint8"),
    "Y": ("sbuf", [128, C], _F),
}
for _t in range(ROUNDS + 1):
    SCRATCH["Qc%d" % _t] = ("sbuf", [128, C], CODES)
    SCRATCH["Qs%d" % _t] = ("sbuf", [128, C], "uint8")
for _t in range(ROUNDS):
    SCRATCH["AL%d" % _t] = ("sbuf", [128, NCH], _F)
    SCRATCH["Ac%d" % _t] = ("sbuf", [128, C], CODES)
    SCRATCH["As%d" % _t] = ("sbuf", [128, C], "uint8")
    SCRATCH["LO%d" % _t] = ("sbuf", [128, 16], "uint16")
    SCRATCH["LS%d" % _t] = ("sbuf", [128, 12], "uint16")
    SCRATCH["LR%d" % _t] = ("sbuf", [128, 12], "uint16")
for _t in range(8):
    SCRATCH["pb%d" % _t] = ("psum", [128, 512], _F)
SEMAPHORES = ["cv", "cs", "ct", "cg", "sent"] + ["d%d" % i for i in range(48)] + ["q%d%d" % (t, h) for t in range(ROUNDS) for h in range(2)] + ["l%d" % t for t in range(ROUNDS)]


def rank_program(g, core, T, topo):
    rank = T.rank_of(core)
    if rank is None:
        return
    n = len(T.cores)
    nxt, prv = T.cores[(rank + 1) % n], T.cores[(rank - 1) % n]
    n_in = len(topo.engines(prv, core))
    rid, pid = topo.addr(nxt)[0], topo.addr(nxt)[1]
    A = AluOpType
    ACT = ActivationFunctionType
    queue = {"v": g.vector, "s": g.scalar, "t": g.tensor, "g": g, "y": g.sync}
    count, seen, hist, need_end = {}, {}, {}, {}

    def view(name, c0, c1, step=1, p0=0, p1=128):
        buf = T[name]
        if step != 1:
            ap = buf[p0:p1, c0:c1:step]
        elif (p0, p1) == (0, 128):
            ap = buf[:, c0:c1]
        else:
            ap = buf[p0:p1, c0:c1]
        return (ap, (name, p0, p1, c0, c1, step))

    def w(name, a=0, b=None, step=1):
        return view(name, a, T[name].shape[1] if b is None else b, step)

    def meet(a, b):
        if a[1] >= b[2] or b[1] >= a[2] or a[3] >= b[4] or b[3] >= a[4]:
            return False
        return not (a[5] == b[5] and a[5] > 1 and (a[3] - b[3]) % a[5])

    def waits(q, reads, writes):
        need = {}
        for kind, rects in (("r", reads), ("w", writes)):
            for r in rects:
                bank = r[0].startswith("pb")
                for hk, hq, hsem, hval, hr in hist.get(r[0], []):
                    if kind == "r" and hk == "r" and not (bank and hq != q):
                        continue
                    if kind == "w" and hq == q and q in "vstg" and not hsem.startswith("d") and (hk == "r" or q == "t"):
                        continue
                    if bank or meet(r, hr):
                        need[hsem] = max(need.get(hsem, 0), hval)
        for s in sorted(need):
            if seen.get((q, s), 0) < need[s]:
                queue[q].wait_ge(T.sem[s], need[s])
                seen[(q, s)] = need[s]
                need_end[s] = max(need_end.get(s, 0), need[s])

    def note(q, sem, val, reads, writes):
        for kind, rects in (("r", reads), ("w", writes)):
            for r in rects:
                lst = hist.setdefault(r[0], [])
                if kind == "w" and r[5] == 1:
                    lst[:] = [h for h in lst if not (h[4][1] >= r[1] and h[4][2] <= r[2] and h[4][3] >= r[3] and h[4][4] <= r[4] and h[1] == q)]
                lst.append((kind, q, sem, val, r))

    def op(q, call, reads, writes):
        reads = [a[1] for a in reads]
        writes = [a[1] for a in writes]
        waits(q, reads, writes)
        sem = "c" + q
        count[sem] = count.get(sem, 0) + 1
        call(queue[q]).then_inc(T.sem[sem], 1)
        note(q, sem, count[sem], reads, writes)

    n_dma = [0]

    def dma(q, out, in_, reads=(), writes=()):
        reads, writes = list(reads), list(writes)
        waits(q, reads, writes)
        sem = "d%d" % n_dma[0]
        n_dma[0] += 1
        count[sem] = 16
        queue[q].dma_start(out, in_).then_inc(T.sem[sem], 16)
        note(q, sem, 16, reads, writes)

    def load(q, name, src, c0=0, c1=None):
        v = w(name, c0, c1)
        dma(q, v[0].bitcast(dt.uint8) if name == "Wc" else v[0], src, (), [v[1]])

    def lands(name, c0, c1, sem, val):
        hist.setdefault(name, []).append(("w", "far", sem, val, (name, 0, 128, c0, c1, 1)))
        count[sem] = max(count.get(sem, 0), val)

    def send(out, in_, rect, sem):
        waits("g", [rect], [])
        count["sent"] = count.get("sent", 0) + len(topo.engines(core, nxt))
        g.remote_dma(out, in_, T.sem[sem], T.sem.sent, pid, rid, topo.mask(core, nxt))

    def fill(ap, val):
        op("v", lambda e: e.memset(ap[0], val), [], [ap])

    def act(out, in_, func=ACT.Copy, scale=1.0, bias=0.0):
        a = scale[0] if isinstance(scale, tuple) else scale
        op("s", lambda e: e.activation(out[0], in_[0], func, bias=bias, scale=a), [in_] + ([scale] if isinstance(scale, tuple) else []), [out])

    def copy(q, out, in_, scale=None):
        if q == "s":
            act(out, in_, ACT.Copy, 1.0 if scale is None else scale)
        elif scale is None:
            op(q, lambda e: e.tensor_copy(out[0], in_[0]), [in_], [out])
        else:
            ts(out, in_, scale, A.mult)

    def ts(out, in_, s1, o1, s2=None, o2=None):
        reads = [in_] + [s for s in (s1, s2) if isinstance(s, tuple)]
        a1 = s1[0] if isinstance(s1, tuple) else s1
        a2 = s2[0] if isinstance(s2, tuple) else s2
        if o2 is None:
            op("v", lambda e: e.tensor_scalar(out[0], in_[0], a1, None, o1), reads, [out])
        else:
            op("v", lambda e: e.tensor_scalar(out[0], in_[0], a1, a2, o1, o2), reads, [out])

    def tt(out, a, b, o):
        op("v", lambda e: e.tensor_tensor(out[0], a[0], b[0], o), [a, b], [out])

    def scan(out, a, b):
        op("v", lambda e: e.tensor_tensor_scan(out[0], a[0], b[0], 0.0, A.mult, A.add), [a, b], [out])

    def turn(out, in_):
        op("v", lambda e: e.transpose(out[0], in_[0]), [in_], [out])

    def gather(q, out, win, off):
        src = win[0].indirect(off[0])
        if q == "s":
            op(q, lambda e: e.activation(out[0], src, ACT.Copy), [win, off], [out])
        else:
            op(q, lambda e: e.tensor_copy(out[0], src), [win, off], [out])

    def quant(c, s, tile, c0, c1, t0):
        qc, qs, x = view(c, c0, c1), view(s, c0, c1), view(tile, t0, t0 + 4 * (c1 - c0))
        op("v", lambda e: e.quantize_mx(qc[0], qs[0], x[0]), [x], [qc, qs])

    bank = [0]

    def product(pairs, rhs, c0, c1):
        out = view("pb%d" % (bank[0] % 8), 0, c1 - c0)
        bank[0] += 1
        rc, rs = view(rhs[0], c0, c1), view(rhs[1], c0, c1)
        for i, (c, s, a) in enumerate(pairs):
            lc, ls = view(c, a, a + 128), view(s, a, a + 128)
            first, last = i == 0, i == len(pairs) - 1
            op("t", lambda e: e.matmul_mx(out[0], lc[0], ls[0], rc[0], rs[0], first, last), [lc, ls, rc, rs], [out])
        return out

    for t in range(ROUNDS):
        for h, (c0, c1) in enumerate(PARTS):
            for name in ("Ac%d" % t, "As%d" % t):
                lands(name, c0, c1, "q%d%d" % (t, h if t else 0), 2 * n_in)
        lands("LR%d" % t, 0, 12, "l%d" % t, n_in)

    load("y", "NX", T.nx[:])
    load("s", "X", T.x[:, 0:4 * NO], 0, 4 * NO)
    load("y", "X", T.x[:, 4 * NO:4 * C], 4 * NO, 4 * C)
    load("s", "UB", T.u[:])
    load("y", "ALI", T.al[:])
    load("y", "Wc", T.wc[:])
    load("s", "Ws", T.ws[:])
    load("y", "VB", T.v[:])

    def iota(out, pattern, base, mult, loose=False):
        if loose:
            op("g", lambda e: e.iota(out[0], pattern, base, mult, allow_small_or_imprecise_dtypes=True), [], [out])
        else:
            op("g", lambda e: e.iota(out[0], pattern, base, mult), [], [out])
    iota(w("PI"), [[1, 1]], 0, 1)
    for b in range(2):
        iota(w("AT", 24 * b, 24 * b + 24), [[128, 3], [0, 2], [1, 4]], 0, 0, True)
    iota(w("LP"), [[16, 8]], 0, 0)
    iota(w("AW"), [[1, C]], 0, 0, True)
    iota(w("CT"), [[0, 2048]], 0, 0, True)
    for b in range(4):
        d = view("CT", 512 * b + b, 512 * b + 512, 4)
        op("g", lambda e: e.affine_select(d[0], d[0], [[-1, 128]], A.not_equal, 64.0, 0, 1), [d], [d])
    fill(w("ZZ"), 0.0)
    ts(w("P15"), w("PI"), 15, A.bitwise_and)
    ts(w("P31"), w("PI"), 31, A.bitwise_and)
    ts(w("M9"), w("P15"), A_ROW, A.is_equal)
    ts(w("PHF"), w("P31"), 4.0, A.mult)
    for ph in range(4):
        act(w("TAB", 192 * ph, 192 * ph + 96), w("AW", ph, C, 4), ACT.Copy, w("M9"))
        copy("s", w("TAB", 192 * ph + 96, 192 * ph + 192), w("ZZ", 0, 96))
    copy("s", w("D0", 0, 768, 2), w("ZZ", 0, 384))
    for name in ("RO", "RR", "EO", "ER", "OAF"):
        copy("s", w(name), w("ZZ", 0, T[name].shape[1]))
    ts(w("AT"), w("AT"), w("PHF"), A.add)
    for name, ratio in (("HE", 2.0), ("HO", 16.0)):
        fill(w(name), ratio)
        fill(w(name, 0, 192, 4), 0.0)
    ts(w("SC"), w("P15"), 0, A.is_equal, 2.0 ** (ODD0 - EVEN0 - 3) - 1.0, A.mult)
    ts(w("PU"), w("PI"), 4, A.logical_shift_right, 1, A.bitwise_and)
    ts(w("E3"), w("P15"), EDGE_ROWS[0], A.is_equal)
    ts(w("E4"), w("P15"), EDGE_ROWS[1], A.is_equal, 17, A.mult)
    ts(w("SC"), w("SC"), 1.0, A.add)
    copy("v", w("PUF"), w("PU"))
    tt(w("LP", 0, 1), w("E3"), w("E4"), A.add)
    ts(w("PLF"), w("PUF"), -1.0, A.mult, 1.0, A.add)
    copy("v", w("LPU"), w("LP"))
    for k in range(1, 4):
        lo, up = 2.0 ** (EVEN0 + k), 2.0 ** (ODD0 + Q2[k])
        ts(w("KC", k, k + 1), w("PUF"), up - lo, A.mult, lo, A.add)

    ts(w("CI"), w("NX"), 9, A.logical_shift_right)
    ts(w("U4"), w("CI"), 4.0, A.mult, -8.0, A.add)
    tt(w("UU"), w("CI"), w("U4"), A.max)
    turn(w("UT"), w("UU"))
    act(w("V2"), w("UT"), ACT.Square)
    act(w("V4"), w("V2"), ACT.Square)
    scan(w("SO"), w("HO"), w("UT"))
    ts(w("NI"), w("NX"), 511, A.bitwise_and)
    turn(w("FD"), w("SO"))
    turn(w("NT"), w("NI"))
    scan(w("SE"), w("HE"), w("V4"))
    tt(w("FD", 96, 192), w("FD", 96, 192), w("FD", 0, 96), A.subtract)
    turn(w("FE"), w("SE"))
    for e in range(3):
        tt(w("ND", e, 192, 4), w("NT", e, 192, 4), w("NT", e + 1, 192, 4), A.subtract)
    tt(w("ND", 3, 192, 4), w("NT", 3, 192, 4), w("AT"), A.subtract)
    tt(w("FE", 96, 192), w("FE", 96, 192), w("FE", 0, 96), A.subtract)
    turn(w("NF"), w("ND"))
    tt(w("NF", 96, 192), w("NF", 96, 192), w("NF", 0, 96), A.subtract)

    def to_row(q, name, e, r):
        dma(q, T.TAB[r:128:16, :], T[name][e:128:4, :], [(name, 0, 128, 0, 192, 1), ("TAB", 16, 128, 0, 768, 1)], [("TAB", r, r + 1, 0, 768, 1)])
    to_row("s", "FD", 3, 2)
    to_row("y", "FE", 3, 0)
    for e in range(4):
        to_row("sysy"[e], "NF", e, 1 + 2 * e)
    act(w("GG"), w("ZZ"), ACT.Identity, 1.0, 1.0)
    copy("s", w("GG", 0, 16 * NCH, 8), w("ZZ", 0, 2 * NCH))
    for t in range(ROUNDS):
        copy("s", w("AL%d" % t, 27, 28), w("ZZ", 0, 1))

    def send_x(t, c0, c1, h):
        for a, b in (("Qc%d", "Ac%d"), ("Qs%d", "As%d")):
            s, d = T[a % t][:, c0:c1], T[b % t][:, c0:c1]
            if a == "Qc%d":
                s, d = s.bitcast(dt.uint8), d.bitcast(dt.uint8)
            send(d, s, (a % t, 0, 128, c0, c1, 1), "q%d%d" % (t, h))

    def quant_x(t, h):
        c0, c1 = PARTS[h]
        quant("Qc%d" % t, "Qs%d" % t, "X", c0, c1, 4 * c0)

    quant_x(0, 0)
    quant_x(0, 1)
    send_x(0, 0, C, 0)
    quant("Uc", "Us", "UB", 0, 128, 0)
    op("v", lambda e: e.tensor_copy(T.Pc[:, 0:128].bitcast(dt.uint32), T.Uc[:, 0:128].bitcast(dt.uint32).indirect(T.LPU[:, 0:8])), [w("Uc"), w("LPU")], [w("Pc")])
    op("v", lambda e: e.tensor_copy(T.Ps[:, 0:128], T.Us[:, 0:128].indirect(T.LPU[:, 0:8])), [w("Us"), w("LPU")], [w("Ps")])
    for name, o, a, b in (("L2O", 0, 0, 14), ("L2O", 14, 0, 2), ("L2R", 0, 14, 24), ("L2R", 10, 14, 16)):
        ts(w(name, o, o + b - a), w("ALI", a, b), 2.0, A.mult)
    ts(w("GG", 5, 16 * NCH, 16), w("ZZ", 0, NCH), w("PLF"), A.add)
    ts(w("GG", 13, 16 * NCH, 16), w("ZZ", 0, NCH), w("PUF"), A.add)
    quant("CTc", "CTs", "CT", 0, 512, 0)

    def score(t, h):
        c0, c1 = PARTS[h]
        return product([("Pc", "Ps", 0)], ("Qc%d" % t, "Qs%d" % t), c0, c1)

    def unpack(src, dst, h, qs):
        c0, c1 = PARTS[h]
        outs = [product([("CTc", "CTs", 128 * b)], src, c0, c1) for b in range(4)]
        return [(qs[b], w(dst, C * b + c0, C * b + c1), outs[b]) for b in range(4)]

    def take(jobs):
        for q, out, ps in jobs:
            copy(q, out, ps, 2.0 ** -6)

    def bits(ps, h):
        c0, c1 = PARTS[h]
        ts(w("D1", 2 * c0, 2 * c1, 2), ps, 0.0, A.is_gt)

    def choose(h):
        c0, c1 = PARTS[h]
        scan(w("TW", 7 + 2 * c0, 7 + 2 * c1), w("D0", 2 * c0, 2 * c1), w("D1", 2 * c0, 2 * c1))

    def edges(h):
        c0, c1 = PARTS[h]
        m, name = c1 - c0, ("EO", "ER")[h]
        for a, b, o in ((0, m, 0), (0, 16, m)):
            copy("s", view(name, o, o + b - a, 1, 0, 32), view("D1", 2 * (c0 + a), 2 * (c0 + b), 2, 0, 32))

    def turns(h, src, dst, p1):
        m = (14, 10)[h]
        first, second = ((0, 14), (8, 22))[h]
        turn(view(dst, 32 * first, 32 * first + 16 * (m + 2), 1, 0, p1), view(src, 0, 16 * (m + 2), 1, 0, p1))
        turn(view(dst, 32 * second, 32 * second + 32, 1, 0, p1), view(src, 16 * (m - 1), 16 * (m + 1), 1, 0, p1))
        turn(view(dst, 32 * second + 32, 32 * second + 32 + 16 * m, 1, 0, p1), view(src, 16, 16 * (m + 1), 1, 0, p1))

    def start():
        p = lambda name, a, b, step: view(name, a, b, step, 0, 32)
        act(p("MA", 0, NCH, 1), p("CE", EDGE_ROWS[0], 32 * NCH, 32), ACT.Identity, 3.0 * 2.0 ** EVEN0, 2.0 ** EVEN0)
        act(p("MB", 0, NCH, 1), p("CE", EDGE_ROWS[1], 32 * NCH, 32), ACT.Identity, 1.0, 1.0)

    def carries(t):
        n2 = 2 * NCH
        p = lambda name, a, b, step, q: view(name, a, b, step, 32 * q, 32 * q + 32)
        masks = (sum(2 ** (ODD0 + k) for k in Q2), sum(2 ** (EVEN0 + k) for k in range(4)))
        for s in range(7):
            q, o = s // 2, s % 2
            q2, o2 = (s + 1) // 2, (s + 1) % 2
            tt(p("YY", 0, NCH, 1, q), p("CH", (0, 18)[o], 32 * NCH, 32, q), p("MM", o, n2, 2, q), A.mult)
            ts(p("MM", o2, n2, 2, q2), p("YY", 0, NCH, 1, q), masks[o], A.bitwise_and)
        for k in range(1, 4):
            ts(w("GG", k, 16 * NCH, 8), w("MM"), w("KC", k, k + 1), A.is_lt)
        ts(w("GG", 4, 16 * NCH, 8), w("MM"), 0.0, A.is_gt)
        scan(w("XS"), w("GG"), w("CH", 1, 32 * NCH, 2))
        new = "AL%d" % t
        tt(w(new, 0, 28, 2), w("XS", 7, 224, 16), w("XS", 239, 448, 16), A.add)
        tt(w(new, 1, 27, 2), w("XS", 247, 448, 16), w("XS", 15, 216, 16), A.add)
        copy("v", w("LS%d" % t), w(new, 16, 28))
        send(T["LR%d" % t][:], T["LS%d" % t][:], ("LS%d" % t, 0, 128, 0, 12, 1), "l%d" % t)
        copy("v", w("LO%d" % t), w(new, 0, 16))

    def layer(h, bs=range(4)):
        z = (("ZOc", "ZOs"), ("ZRc", "ZRs"))[h]
        m = (NO, NR)[h]
        return [product([("Wc", "Ws", 128 * b), ("CTc", "CTs", 128 * b)], z, 0, m) for b in bs]

    def state(h, outs, qs, bs=range(4)):
        c0, c1 = PARTS[h]
        for b in bs:
            copy(qs[b], w("X", 4 * c0 + b, 4 * c1, 4), outs[b], 2.0 ** -6)

    def addresses_out():
        copy("v", w("OAF", 0, 14), w("AL%d" % (ROUNDS - 1), 0, 14))
        copy("v", w("OAF", 14, 24), w("LR%d" % (ROUNDS - 1), 0, 10))
        turn(w("OAT"), w("OAF"))
        for k in range(8):
            p0 = 32 * (k // 2)
            dma("y", T.oa[k:k + 1, :], T.OAT[p0:p0 + 24, 16 * (k % 2):16 * (k % 2) + 16], [("OAT", p0, p0 + 24, 0, 32, 1)])

    sa = score(0, 0)
    sb = score(0, 1)
    for t in range(ROUNDS):
        last = t + 1 == ROUNDS
        fa = unpack(("Qc%d" % t, "Qs%d" % t), "FO", 0, "ssss")
        if t == 0:
            bits(sa, 0)
            edges(0)
            bits(sb, 1)
            edges(1)
            for ph in range(4):
                copy("sv"[ph % 2], w("D1", 2 * ph + 1, 768, 8), w("TAB", 192 * ph, 192 * ph + 96), w("SC"))
                copy("vs"[ph % 2], w("D0", 2 * ph + 1, 768, 8), w("TAB", 192 * ph + 96, 192 * ph + 192), w("SC"))
            choose(0)
            turns(0, "EO", "CE", 32)
        else:
            bits(sb, 1)
            edges(1)
        choose(1)
        gather("s", w("RO", 0, 240), w("TW", 8, 776), w("L2O", 0, 15))
        gather("v", w("RR", 0, 176), w("TW", 8, 776), w("L2R", 0, 11))
        turns(1, "ER", "CE", 32)
        start()
        turns(1, "RR", "CH", 128)
        tt(view("MM", 0, 2 * NCH, 2, 0, 32), view("MA", 0, NCH, 1, 0, 32), view("MB", 0, NCH, 1, 0, 32), A.mult)
        turns(0, "RO", "CH", 128)
        take(fa)
        take(unpack(("Qc%d" % t, "Qs%d" % t), "FO", 1, "ssss"))
        carries(t)
        take(unpack(("Ac%d" % t, "As%d" % t), "FP", 0, "ssss"))
        for b in range(4):
            gather("vsvs"[b], w("ZO", b, 4 * NO, 4), w("FO", C * b, C * b + C), w("LO%d" % t, 0, 14))
        quant("ZOc", "ZOs", "ZO", 0, NO, 0)
        take(unpack(("Ac%d" % t, "As%d" % t), "FP", 1, "vsvs"))
        outs = layer(0)
        if t == 0:
            quant("Vc", "Vs", "VB", 0, 128, 0)
        if not last:
            ts(w("L2O", 0, 16), w("AL%d" % t, 0, 16), 2.0, A.mult)
        for b in range(4):
            gather("vsvs"[b], w("ZR", b, 4 * NR, 4), w("FP", C * b, C * b + C), w("LR%d" % t, 0, 10))
        quant("ZRc", "ZRs", "ZR", 0, NR, 0)
        outs2 = layer(1, (0, 1))
        if last:
            addresses_out()
        state(0, outs, "svsv")
        quant_x(t + 1, 0)
        if not last:
            send_x(t + 1, 0, NO, 0)
            sa = score(t + 1, 0)
            ts(w("L2R", 0, 12), w("LR%d" % t), 2.0, A.mult)
        outs2 += layer(1, (2, 3))
        if last:
            state(1, outs2, "svsv")
        else:
            state(1, outs2, "svss", (0, 1))
            bits(sa, 0)
            edges(0)
            choose(0)
            state(1, outs2, "svss", (2, 3))
            turns(0, "EO", "CE", 32)
        quant_x(t + 1, 1)
        if not last:
            send_x(t + 1, NO, C, 1)
            sb = score(t + 1, 1)

    qc, qs = "Qc%d" % ROUNDS, "Qs%d" % ROUNDS
    for h, (c0, c1) in enumerate(PARTS):
        out = product([("Vc", "Vs", 0)], (qc, qs), c0, c1)
        dma("ys"[h], T.oc[:, 4 * c0:4 * c1], T[qc][:, c0:c1].bitcast(dt.uint8), [(qc, 0, 128, c0, c1, 1)])
        copy("sv"[h], w("Y", c0, c1), out)
        dma("ys"[h], T.y[:, c0:c1], T.Y[:, c0:c1], [("Y", 0, 128, c0, c1, 1)])
    for k in range(4):
        dma("y", T.osc[4 * k:4 * k + 4, :], T[qs][32 * k:32 * k + 4, :], [(qs, 0, 128, 0, C, 1)])

    for s in sorted(count):
        if need_end.get(s, 0) < count[s]:
            g.wait_ge(T.sem[s], count[s])
